import numpy as np
import ml_dtypes


def mxq(x, axis, fmt="e4m3"):
    dtype, down = {"e4m3": (ml_dtypes.float8_e4m3fn, 7), "e5m2": (ml_dtypes.float8_e5m2, 14)}[fmt]
    v = np.moveaxis(np.asarray(x, np.float32).astype(ml_dtypes.bfloat16).astype(np.float64), axis, -1)
    blocks = v.reshape(v.shape[:-1] + (-1, 32))
    amax = np.abs(blocks).max(-1, keepdims=True)
    byte = np.maximum(np.where(amax > 0, np.frexp(amax)[1] - 1 + 127, 0) - down, 1)
    scale = np.exp2(byte - 127.0)
    codes = (blocks / scale).astype(np.float32).astype(dtype).astype(np.float64)
    return np.moveaxis((codes * scale).reshape(v.shape), -1, axis)


WIDE = False


def mx_kscale(k):
    if not WIDE:
        return np.ones(k)
    levels = np.array([10, -10, 5, -5, 0])
    if k % 512:
        return np.exp2(np.random.permutation(np.resize(levels, k // 32))).repeat(32)
    a = np.empty((k // 512, 16))
    for p in range(k // 512):
        a[p, :8] = np.random.permutation(np.resize(levels, 8))
        for g in range(8):
            far = levels[np.abs(levels - a[p, g]) >= 10]
            a[p, g + 8] = far[np.random.randint(len(far))]
    return np.exp2(a.ravel()).repeat(32)


def f64(x):
    return np.asarray(x).astype(np.float64)


def striped8(idx):
    return np.concatenate([v.reshape(-1, 16).T for v in idx]).astype(np.uint16)


def unstriped8(offs):
    return np.stack([offs[16 * g:16 * g + 16].T.reshape(-1) for g in range(8)]).astype(np.int64)


E2M1 = np.array([0.0, 0.5, 1.0, 1.5, 2.0, 3.0, 4.0, 6.0, -0.0, -0.5, -1.0, -1.5, -2.0, -3.0, -4.0, -6.0])


def pack_weight(w, fmt):
    k, n = w.shape
    w = f64(np.asarray(w, np.float32).astype(ml_dtypes.bfloat16)).reshape(k // 32, 32, n)
    amax = np.abs(w).max(1)
    if fmt == "e4m3":
        byte = np.frexp(amax)[1] - 1 + 127 - 7
    else:
        mant, ex = np.frexp(amax / 6.0)
        byte = np.where(mant > 0.5, ex, ex - 1) + 127
    byte = np.clip(np.where(amax > 0, byte, 1), 1, 254)
    scaled = (w * np.exp2(127.0 - byte)[:, None, :]).reshape(k, n).astype(np.float32)
    by_word = np.ascontiguousarray(scaled.reshape(k // 512, 128, 4, n).transpose(0, 1, 3, 2))
    if fmt == "e4m3":
        words = by_word.astype(ml_dtypes.float8_e4m3fn).view(np.uint8)
    else:
        c = by_word.astype(ml_dtypes.float4_e2m1fn).view(np.uint8) & 0xF
        words = (c[..., 0::2] | (c[..., 1::2] << 4)).reshape(k // 512, 128, 2 * n)
    return np.ascontiguousarray(words), np.ascontiguousarray(byte.astype(np.uint8).reshape(k // 512, 16, n))


def unpack_weight(words, scales, fmt):
    g, _, n = scales.shape
    words = np.ascontiguousarray(words).reshape(g, 128, n, -1)
    if fmt == "e4m3":
        vals = words.view(ml_dtypes.float8_e4m3fn).astype(np.float64)
    else:
        nib = np.empty((g, 128, n, 4), np.uint8)
        nib[..., 0::2] = words & 0xF
        nib[..., 1::2] = words >> 4
        vals = E2M1[nib]
    vals = vals * np.repeat(np.exp2(scales.astype(np.float64) - 127.0), 8, axis=1)[..., None]
    return vals.transpose(0, 1, 3, 2).reshape(g * 512, n)


K, M, T, S = 2048, 128, 1024, 512


def setup_inputs():
    n = np.random.standard_normal
    s = mx_kscale(K)[:, None]
    p_w = pack_weight(n((K, M)) / np.sqrt(K) / s, "e4m3")
    return {
        "xT": (n((K, T)) * s).astype(np.float32),
        "w_words": p_w[0],
        "w_scales": p_w[1],
        "wgt": np.repeat(np.random.uniform(0.5, 2.0, (8, S)), 16, axis=0).astype(np.float32),
        "r": (n((128, 512))).astype(np.float32),
        "offs": striped8(np.stack([np.random.permutation(T)[:S] for _ in range(8)])),
    }


def reference(xT, w_words, w_scales, wgt, r, offs):
    idx = unstriped8(offs)
    group = np.arange(K) % 512 // 64
    xg = f64(wgt)[np.arange(K) // 4 % 128] * f64(xT)[np.arange(K)[:, None], idx[group]]
    xT_ = mxq(xg, 0, "e4m3")
    w_ = unpack_weight(w_words, w_scales, "e4m3")
    y = w_.T @ xT_
    return f64(r) + y

@@ -1,0 +1,140 @@
+from contextlib import ExitStack
+
+import concourse.mybir as mybir
+
+K, M, T, S = 2048, 128, 1024, 512
+FLOPS = 2 * K * M * S
+
+F32 = mybir.dt.float32
+BF16 = mybir.dt.bfloat16
+I32 = mybir.dt.int32
+U32 = mybir.dt.uint32
+U16 = mybir.dt.uint16
+U8 = mybir.dt.uint8
+FP8X4 = mybir.dt.float8_e4m3fn_x4
+MULT, ADD = mybir.AluOpType.mult, mybir.AluOpType.add
+
+P = 128
+PASSES = K // 512
+WIDE = [(0, 256), (256, 512)]
+LAST = [(0, 256), (256, 384), (384, 512)]
+
+
+def tile_list_heads_res_kernel(tc, xT, w_words, w_scales, wgt, r, offs, out):
+    nc = tc.nc
+    with ExitStack() as ctx:
+        keep = ctx.enter_context(tc.tile_pool(name="keep", bufs=1))
+        psum = ctx.enter_context(tc.psum_pool(name="psum", bufs=1))
+
+        lists = keep.tile([P, S // 16], U16, name="lists")
+        nc.sync.dma_start(lists[:], offs)
+
+        factors = {}
+        for c0, c1 in WIDE:
+            factors[c0] = keep.tile([P, c1 - c0], F32, name=f"factors{c0}")
+            nc.scalar.dma_start(out=factors[c0][:], in_=wgt[:, c0:c1])
+
+        w_s = keep.tile([P, PASSES, M], U8, name="w_s", align_bytes=64)
+        nc.vector.memset(w_s[:].rearrange("p a n -> p (a n)").bitcast(I32), 0)
+
+        w_c = keep.tile([P, PASSES, M], U32, name="w_c", align_bytes=64)
+        res = keep.tile([P, S], F32, name="res")
+        planes = {}
+        for a in range(PASSES):
+            rows = xT[512 * a : 512 * (a + 1), :].rearrange("(p i) t -> p i t", i=4)
+            for i in range(4):
+                planes[a, i] = keep.tile([P, T], F32, name=f"plane{a}_{i}")
+                nc.sync.dma_start(out=planes[a, i][:], in_=rows[:, i, :])
+            if a == 0:
+                for q in range(4):
+                    nc.sync.dma_start(
+                        out=w_s[32 * q : 32 * q + 4, :, :].bitcast(I32),
+                        in_=w_scales[:, 4 * q : 4 * q + 4, :].rearrange("a q n -> q a n").bitcast(I32),
+                    )
+            if a == 2:
+                nc.sync.dma_start(
+                    out=w_c[:].bitcast(I32),
+                    in_=w_words.rearrange("a p n t -> p a (n t)").bitcast(I32),
+                )
+        nc.sync.dma_start(out=res[:], in_=r)
+
+        picked = {}
+        packed = {}
+        codes = {}
+        scales = {}
+        acc = {}
+        for a in range(PASSES):
+            for c0, c1 in LAST if a == 3 else WIDE:
+                picked[a, c0] = keep.tile([P, 4, c1 - c0], F32, name=f"picked{a}_{c0}")
+            packed[a] = keep.tile([P, S, 4], BF16, name=f"packed{a}", align_bytes=64)
+            codes[a] = keep.tile([P, S], U32, name=f"codes{a}", align_bytes=64)
+            scales[a] = keep.tile([P, S], U8, name=f"scales{a}", align_bytes=64)
+        for c0, c1 in LAST:
+            acc[c0] = psum.tile([M, c1 - c0], F32, name=f"acc{c0}")
+
+        def gather(a, i, c0, c1):
+            f0 = 0 if c0 < 256 else 256
+            nc.vector.tensor_tensor(
+                picked[a, c0][:, i, :],
+                planes[a, i][:].indirect(lists[:, c0 // 16 : c1 // 16]),
+                factors[f0][:, c0 - f0 : c1 - f0],
+                MULT,
+            )
+
+        def interleave(a, c0, c1):
+            nc.scalar.copy(
+                out=packed[a][:, c0:c1, :].rearrange("p (c i) t -> p c t i", i=4),
+                in_=picked[a, c0][:].rearrange("p t (c i) -> p c t i", i=4),
+            )
+
+        def quantize(a, c0, c1):
+            nc.vector.quantize_mx(
+                out=codes[a][:, c0:c1].bitcast(FP8X4),
+                scales=scales[a][:, c0:c1],
+                in_=packed[a][:, c0:c1, :].rearrange("p c t -> p (c t)"),
+            )
+
+        def multiply(a, c0, c1):
+            nc.tensor.matmul_mx(
+                out=acc[c0][:],
+                lhsT=w_c[:, a, :].bitcast(FP8X4),
+                lhsT_scale=w_s[:, a, :],
+                rhs=codes[a][:, c0:c1].bitcast(FP8X4),
+                rhs_scale=scales[a][:, c0:c1],
+                start=(a == 0),
+                stop=(a == PASSES - 1),
+            )
+
+        def finish(c0, c1):
+            done = keep.tile([M, c1 - c0], F32, name=f"done{c0}")
+            nc.vector.tensor_tensor(done[:], acc[c0][:], res[:, c0:c1], ADD)
+            nc.sync.dma_start(out=out[:, c0:c1], in_=done[:])
+
+        for a in range(PASSES - 1):
+            for i in range(4):
+                for c0, c1 in WIDE:
+                    gather(a, i, c0, c1)
+                if a > 0 and i == 2:
+                    quantize(a - 1, 0, S)
+                    for c0, c1 in LAST:
+                        multiply(a - 1, c0, c1)
+            for c0, c1 in WIDE:
+                interleave(a, c0, c1)
+        c_a, c_b, c_c = LAST
+        for i in range(4):
+            gather(3, i, *c_a)
+        interleave(3, *c_a)
+        quantize(2, 0, S)
+        for c0, c1 in LAST:
+            multiply(2, c0, c1)
+        for i in range(4):
+            gather(3, i, *c_b)
+        interleave(3, *c_b)
+        for i in range(4):
+            gather(3, i, *c_c)
+        interleave(3, *c_c)
+        for c0, c1 in LAST:
+            quantize(3, c0, c1)
+            multiply(3, c0, c1)
+        for c0, c1 in LAST:
+            finish(c0, c1)

@@ -16,8 +16,8 @@ MULT, ADD = mybir.AluOpType.mult, mybir.AluOpType.add
 
 P = 128
 PASSES = K // 512
-WIDE = [(0, 256), (256, 512)]
-LAST = [(0, 256), (256, 384), (384, 512)]
+CUTS = {0: [(0, 128), (128, 512)], 1: [(0, 128), (128, 512)], 2: [(0, 128), (128, 512)], 3: [(0, 384), (384, 512)]}
+BANKS = [(0, 256), (256, 384), (384, 512)]
 
 
 def tile_list_heads_res_kernel(tc, xT, w_words, w_scales, wgt, r, offs, out):
@@ -28,34 +28,31 @@ def tile_list_heads_res_kernel(tc, xT, w_words, w_scales, wgt, r, offs, out):
 
         lists = keep.tile([P, S // 16], U16, name="lists")
         nc.sync.dma_start(lists[:], offs)
+        factors = keep.tile([P, S], F32, name="factors")
+        nc.scalar.dma_start(out=factors[:, 0:128], in_=wgt[:, 0:128])
 
-        factors = {}
-        for c0, c1 in WIDE:
-            factors[c0] = keep.tile([P, c1 - c0], F32, name=f"factors{c0}")
-            nc.scalar.dma_start(out=factors[c0][:], in_=wgt[:, c0:c1])
-
-        w_s = keep.tile([P, PASSES, M], U8, name="w_s", align_bytes=64)
-        nc.vector.memset(w_s[:].rearrange("p a n -> p (a n)").bitcast(I32), 0)
-
-        w_c = keep.tile([P, PASSES, M], U32, name="w_c", align_bytes=64)
-        res = keep.tile([P, S], F32, name="res")
         planes = {}
         for a in range(PASSES):
             rows = xT[512 * a : 512 * (a + 1), :].rearrange("(p i) t -> p i t", i=4)
             for i in range(4):
                 planes[a, i] = keep.tile([P, T], F32, name=f"plane{a}_{i}")
                 nc.sync.dma_start(out=planes[a, i][:], in_=rows[:, i, :])
-            if a == 0:
-                for q in range(4):
-                    nc.sync.dma_start(
-                        out=w_s[32 * q : 32 * q + 4, :, :].bitcast(I32),
-                        in_=w_scales[:, 4 * q : 4 * q + 4, :].rearrange("a q n -> q a n").bitcast(I32),
-                    )
-            if a == 2:
-                nc.sync.dma_start(
-                    out=w_c[:].bitcast(I32),
-                    in_=w_words.rearrange("a p n t -> p a (n t)").bitcast(I32),
-                )
+                if a == 0 and i == 0:
+                    nc.sync.dma_start(out=factors[:, 128:512], in_=wgt[:, 128:512])
+
+        w_s = keep.tile([P, PASSES, M], U8, name="w_s", align_bytes=64)
+        nc.vector.memset(w_s[:].rearrange("p a n -> p (a n)").bitcast(I32), 0)
+        for q in range(4):
+            nc.sync.dma_start(
+                out=w_s[32 * q : 32 * q + 4, :, :].bitcast(I32),
+                in_=w_scales[:, 4 * q : 4 * q + 4, :].rearrange("a q n -> q a n").bitcast(I32),
+            )
+        w_c = keep.tile([P, PASSES, M], U32, name="w_c", align_bytes=64)
+        nc.sync.dma_start(
+            out=w_c[:].bitcast(I32),
+            in_=w_words.rearrange("a p n t -> p a (n t)").bitcast(I32),
+        )
+        res = keep.tile([P, S], F32, name="res")
         nc.sync.dma_start(out=res[:], in_=r)
 
         picked = {}
@@ -64,25 +61,24 @@ def tile_list_heads_res_kernel(tc, xT, w_words, w_scales, wgt, r, offs, out):
         scales = {}
         acc = {}
         for a in range(PASSES):
-            for c0, c1 in LAST if a == 3 else WIDE:
+            for c0, c1 in CUTS[a]:
                 picked[a, c0] = keep.tile([P, 4, c1 - c0], F32, name=f"picked{a}_{c0}")
             packed[a] = keep.tile([P, S, 4], BF16, name=f"packed{a}", align_bytes=64)
             codes[a] = keep.tile([P, S], U32, name=f"codes{a}", align_bytes=64)
             scales[a] = keep.tile([P, S], U8, name=f"scales{a}", align_bytes=64)
-        for c0, c1 in LAST:
+        for c0, c1 in BANKS:
             acc[c0] = psum.tile([M, c1 - c0], F32, name=f"acc{c0}")
 
         def gather(a, i, c0, c1):
-            f0 = 0 if c0 < 256 else 256
             nc.vector.tensor_tensor(
                 picked[a, c0][:, i, :],
                 planes[a, i][:].indirect(lists[:, c0 // 16 : c1 // 16]),
-                factors[f0][:, c0 - f0 : c1 - f0],
+                factors[:, c0:c1],
                 MULT,
             )
 
-        def interleave(a, c0, c1):
-            nc.scalar.copy(
+        def interleave(copy, a, c0, c1):
+            copy(
                 out=packed[a][:, c0:c1, :].rearrange("p (c i) t -> p c t i", i=4),
                 in_=picked[a, c0][:].rearrange("p t (c i) -> p c t i", i=4),
             )
@@ -112,29 +108,27 @@ def tile_list_heads_res_kernel(tc, xT, w_words, w_scales, wgt, r, offs, out):
 
         for a in range(PASSES - 1):
             for i in range(4):
-                for c0, c1 in WIDE:
+                for c0, c1 in CUTS[a]:
                     gather(a, i, c0, c1)
                 if a > 0 and i == 2:
                     quantize(a - 1, 0, S)
-                    for c0, c1 in LAST:
-                        multiply(a - 1, c0, c1)
-            for c0, c1 in WIDE:
-                interleave(a, c0, c1)
-        c_a, c_b, c_c = LAST
+            for c0, c1 in CUTS[a]:
+                interleave(nc.scalar.copy, a, c0, c1)
         for i in range(4):
-            gather(3, i, *c_a)
-        interleave(3, *c_a)
-        quantize(2, 0, S)
-        for c0, c1 in LAST:
-            multiply(2, c0, c1)
+            gather(3, i, 0, 384)
+            if i == 2:
+                quantize(2, 0, S)
+        interleave(nc.scalar.copy, 3, 0, 384)
+        for a in range(PASSES - 1):
+            for c0, c1 in BANKS:
+                multiply(a, c0, c1)
         for i in range(4):
-            gather(3, i, *c_b)
-        interleave(3, *c_b)
-        for i in range(4):
-            gather(3, i, *c_c)
-        interleave(3, *c_c)
-        for c0, c1 in LAST:
-            quantize(3, c0, c1)
+            gather(3, i, 384, 512)
+        interleave(nc.vector.tensor_copy, 3, 384, 512)
+        quantize(3, 0, 256)
+        quantize(3, 256, 384)
+        quantize(3, 384, 512)
+        for c0, c1 in BANKS:
             multiply(3, c0, c1)
-        for c0, c1 in LAST:
+        for c0, c1 in BANKS:
             finish(c0, c1)

@@ -78,9 +78,10 @@ def tile_list_heads_res_kernel(tc, xT, w_words, w_scales, wgt, r, offs, out):
             )
 
         def interleave(copy, a, c0, c1):
+            p0 = max(start for start, stop in CUTS[a] if start <= c0)
             copy(
                 out=packed[a][:, c0:c1, :].rearrange("p (c i) t -> p c t i", i=4),
-                in_=picked[a, c0][:].rearrange("p t (c i) -> p c t i", i=4),
+                in_=picked[a, p0][:, :, c0 - p0 : c1 - p0].rearrange("p t (c i) -> p c t i", i=4),
             )
 
         def quantize(a, c0, c1):
@@ -116,16 +117,17 @@ def tile_list_heads_res_kernel(tc, xT, w_words, w_scales, wgt, r, offs, out):
                 interleave(nc.scalar.copy, a, c0, c1)
         for i in range(4):
             gather(3, i, 0, 384)
-            if i == 2:
-                quantize(2, 0, S)
-        interleave(nc.scalar.copy, 3, 0, 384)
+        quantize(2, 0, S)
+        interleave(nc.scalar.copy, 3, 0, 256)
+        interleave(nc.scalar.copy, 3, 256, 384)
         for a in range(PASSES - 1):
             for c0, c1 in BANKS:
                 multiply(a, c0, c1)
         for i in range(4):
             gather(3, i, 384, 512)
-        interleave(nc.vector.tensor_copy, 3, 384, 512)
         quantize(3, 0, 256)
+        interleave(nc.vector.tensor_copy, 3, 384, 448)
+        interleave(nc.scalar.copy, 3, 448, 512)
         quantize(3, 256, 384)
         quantize(3, 384, 512)
         for c0, c1 in BANKS:

@@ -115,22 +115,21 @@ def tile_list_heads_res_kernel(tc, xT, w_words, w_scales, wgt, r, offs, out):
                     quantize(a - 1, 0, S)
             for c0, c1 in CUTS[a]:
                 interleave(nc.scalar.copy, a, c0, c1)
-        for i in range(4):
+        for i in range(3):
             gather(3, i, 0, 384)
+            gather(3, i, 384, 512)
         quantize(2, 0, S)
-        interleave(nc.scalar.copy, 3, 0, 256)
-        interleave(nc.scalar.copy, 3, 256, 384)
         for a in range(PASSES - 1):
             for c0, c1 in BANKS:
                 multiply(a, c0, c1)
-        for i in range(4):
-            gather(3, i, 384, 512)
-        quantize(3, 0, 256)
-        interleave(nc.vector.tensor_copy, 3, 384, 448)
-        interleave(nc.scalar.copy, 3, 448, 512)
-        quantize(3, 256, 384)
-        quantize(3, 384, 512)
-        for c0, c1 in BANKS:
+        gather(3, 3, 0, 384)
+        interleave(nc.scalar.copy, 3, 0, 256)
+        gather(3, 3, 384, 512)
+        interleave(nc.vector.tensor_copy, 3, 256, 384)
+        interleave(nc.vector.tensor_copy, 3, 384, 512)
+        ends = [BANKS[1], BANKS[0], BANKS[2]]
+        for c0, c1 in ends:
+            quantize(3, c0, c1)
             multiply(3, c0, c1)
-        for c0, c1 in BANKS:
+        for c0, c1 in ends:
             finish(c0, c1)

@@ -27,7 +27,6 @@ def tile_list_heads_res_kernel(tc, xT, w_words, w_scales, wgt, r, offs, out):
         psum = ctx.enter_context(tc.psum_pool(name="psum", bufs=1))
 
         lists = keep.tile([P, S // 16], U16, name="lists")
-        nc.sync.dma_start(lists[:], offs)
         factors = keep.tile([P, S], F32, name="factors")
         nc.scalar.dma_start(out=factors[:, 0:128], in_=wgt[:, 0:128])
 
@@ -38,6 +37,7 @@ def tile_list_heads_res_kernel(tc, xT, w_words, w_scales, wgt, r, offs, out):
                 planes[a, i] = keep.tile([P, T], F32, name=f"plane{a}_{i}")
                 nc.sync.dma_start(out=planes[a, i][:], in_=rows[:, i, :])
                 if a == 0 and i == 0:
+                    nc.sync.dma_start(lists[:], offs)
                     nc.sync.dma_start(out=factors[:, 128:512], in_=wgt[:, 128:512])
 
         w_s = keep.tile([P, PASSES, M], U8, name="w_s", align_bytes=64)
@@ -126,7 +126,8 @@ def tile_list_heads_res_kernel(tc, xT, w_words, w_scales, wgt, r, offs, out):
         interleave(nc.scalar.copy, 3, 0, 256)
         gather(3, 3, 384, 512)
         interleave(nc.vector.tensor_copy, 3, 256, 384)
-        interleave(nc.vector.tensor_copy, 3, 384, 512)
+        interleave(nc.vector.tensor_copy, 3, 384, 448)
+        interleave(nc.scalar.copy, 3, 448, 512)
         ends = [BANKS[1], BANKS[0], BANKS[2]]
         for c0, c1 in ends:
             quantize(3, c0, c1)

from contextlib import ExitStack

import concourse.mybir as mybir

K, M, T, S = 2048, 128, 1024, 512
FLOPS = 2 * K * M * S

F32 = mybir.dt.float32
BF16 = mybir.dt.bfloat16
I32 = mybir.dt.int32
U32 = mybir.dt.uint32
U16 = mybir.dt.uint16
U8 = mybir.dt.uint8
FP8X4 = mybir.dt.float8_e4m3fn_x4
MULT, ADD = mybir.AluOpType.mult, mybir.AluOpType.add

P = 128
PASSES = K // 512
CUTS = {0: [(0, 128), (128, 512)], 1: [(0, 128), (128, 512)], 2: [(0, 128), (128, 512)], 3: [(0, 384), (384, 512)]}
BANKS = [(0, 256), (256, 384), (384, 512)]


def tile_list_heads_res_kernel(tc, xT, w_words, w_scales, wgt, r, offs, out):
    nc = tc.nc
    with ExitStack() as ctx:
        keep = ctx.enter_context(tc.tile_pool(name="keep", bufs=1))
        psum = ctx.enter_context(tc.psum_pool(name="psum", bufs=1))

        lists = keep.tile([P, S // 16], U16, name="lists")
        factors = keep.tile([P, S], F32, name="factors")
        nc.scalar.dma_start(out=factors[:, 0:128], in_=wgt[:, 0:128])

        planes = {}
        for a in range(PASSES):
            rows = xT[512 * a : 512 * (a + 1), :].rearrange("(p i) t -> p i t", i=4)
            for i in range(4):
                planes[a, i] = keep.tile([P, T], F32, name=f"plane{a}_{i}")
                nc.sync.dma_start(out=planes[a, i][:], in_=rows[:, i, :])
                if a == 0 and i == 0:
                    nc.sync.dma_start(lists[:], offs)
                    nc.sync.dma_start(out=factors[:, 128:512], in_=wgt[:, 128:512])

        w_s = keep.tile([P, PASSES, M], U8, name="w_s", align_bytes=64)
        nc.vector.memset(w_s[:].rearrange("p a n -> p (a n)").bitcast(I32), 0)
        for q in range(4):
            nc.sync.dma_start(
                out=w_s[32 * q : 32 * q + 4, :, :].bitcast(I32),
                in_=w_scales[:, 4 * q : 4 * q + 4, :].rearrange("a q n -> q a n").bitcast(I32),
            )
        w_c = keep.tile([P, PASSES, M], U32, name="w_c", align_bytes=64)
        nc.sync.dma_start(
            out=w_c[:].bitcast(I32),
            in_=w_words.rearrange("a p n t -> p a (n t)").bitcast(I32),
        )
        res = keep.tile([P, S], F32, name="res")
        nc.sync.dma_start(out=res[:], in_=r)

        picked = {}
        packed = {}
        codes = {}
        scales = {}
        acc = {}
        for a in range(PASSES):
            for c0, c1 in CUTS[a]:
                picked[a, c0] = keep.tile([P, 4, c1 - c0], F32, name=f"picked{a}_{c0}")
            packed[a] = keep.tile([P, S, 4], BF16, name=f"packed{a}", align_bytes=64)
            codes[a] = keep.tile([P, S], U32, name=f"codes{a}", align_bytes=64)
            scales[a] = keep.tile([P, S], U8, name=f"scales{a}", align_bytes=64)
        for c0, c1 in BANKS:
            acc[c0] = psum.tile([M, c1 - c0], F32, name=f"acc{c0}")

        def gather(a, i, c0, c1):
            nc.vector.tensor_tensor(
                picked[a, c0][:, i, :],
                planes[a, i][:].indirect(lists[:, c0 // 16 : c1 // 16]),
                factors[:, c0:c1],
                MULT,
            )

        def interleave(copy, a, c0, c1):
            p0 = max(start for start, stop in CUTS[a] if start <= c0)
            copy(
                out=packed[a][:, c0:c1, :].rearrange("p (c i) t -> p c t i", i=4),
                in_=picked[a, p0][:, :, c0 - p0 : c1 - p0].rearrange("p t (c i) -> p c t i", i=4),
            )

        def quantize(a, c0, c1):
            nc.vector.quantize_mx(
                out=codes[a][:, c0:c1].bitcast(FP8X4),
                scales=scales[a][:, c0:c1],
                in_=packed[a][:, c0:c1, :].rearrange("p c t -> p (c t)"),
            )

        def multiply(a, c0, c1):
            nc.tensor.matmul_mx(
                out=acc[c0][:],
                lhsT=w_c[:, a, :].bitcast(FP8X4),
                lhsT_scale=w_s[:, a, :],
                rhs=codes[a][:, c0:c1].bitcast(FP8X4),
                rhs_scale=scales[a][:, c0:c1],
                start=(a == 0),
                stop=(a == PASSES - 1),
            )

        def finish(c0, c1):
            done = keep.tile([M, c1 - c0], F32, name=f"done{c0}")
            nc.vector.tensor_tensor(done[:], acc[c0][:], res[:, c0:c1], ADD)
            nc.sync.dma_start(out=out[:, c0:c1], in_=done[:])

        for a in range(PASSES - 1):
            for i in range(4):
                for c0, c1 in CUTS[a]:
                    gather(a, i, c0, c1)
                if a > 0 and i == 2:
                    quantize(a - 1, 0, S)
            for c0, c1 in CUTS[a]:
                interleave(nc.scalar.copy, a, c0, c1)
        for i in range(3):
            gather(3, i, 0, 384)
            gather(3, i, 384, 512)
        quantize(2, 0, S)
        for a in range(PASSES - 1):
            for c0, c1 in BANKS:
                multiply(a, c0, c1)
        gather(3, 3, 0, 384)
        interleave(nc.scalar.copy, 3, 0, 256)
        gather(3, 3, 384, 512)
        interleave(nc.vector.tensor_copy, 3, 256, 384)
        interleave(nc.vector.tensor_copy, 3, 384, 448)
        interleave(nc.scalar.copy, 3, 448, 512)
        ends = [BANKS[1], BANKS[0], BANKS[2]]
        for c0, c1 in ends:
            quantize(3, c0, c1)
            multiply(3, c0, c1)
        for c0, c1 in ends:
            finish(c0, c1)
